import numpy as np
import ml_dtypes


def mxq(x, axis, fmt="e4m3"):
    dtype, down = {"e4m3": (ml_dtypes.float8_e4m3fn, 7), "e5m2": (ml_dtypes.float8_e5m2, 14)}[fmt]
    v = np.moveaxis(np.asarray(x, np.float32).astype(ml_dtypes.bfloat16).astype(np.float64), axis, -1)
    blocks = v.reshape(v.shape[:-1] + (-1, 32))
    amax = np.abs(blocks).max(-1, keepdims=True)
    byte = np.maximum(np.where(amax > 0, np.frexp(amax)[1] - 1 + 127, 0) - down, 1)
    scale = np.exp2(byte - 127.0)
    codes = (blocks / scale).astype(np.float32).astype(dtype).astype(np.float64)
    return np.moveaxis((codes * scale).reshape(v.shape), -1, axis)


WIDE = False


def mx_kscale(k):
    if not WIDE:
        return np.ones(k)
    levels = np.array([30, -30])
    if k % 512:
        return np.exp2(np.random.permutation(np.resize(levels, k // 32))).repeat(32)
    a = np.empty((k // 512, 16))
    for p in range(k // 512):
        a[p, :8] = np.random.permutation(np.resize(levels, 8))
        for g in range(8):
            far = levels[np.abs(levels - a[p, g]) >= 10]
            a[p, g + 8] = far[np.random.randint(len(far))]
    return np.exp2(a.ravel()).repeat(32)


def f64(x):
    return np.asarray(x).astype(np.float64)


def striped(idx):
    return np.tile(np.asarray(idx).reshape(-1, 16).T, (8, 1)).astype(np.uint16)


def unstriped(offs):
    return offs[:16].T.reshape(-1).astype(np.int64)


E2M1 = np.array([0.0, 0.5, 1.0, 1.5, 2.0, 3.0, 4.0, 6.0, -0.0, -0.5, -1.0, -1.5, -2.0, -3.0, -4.0, -6.0])


def pack_weight(w, fmt):
    k, n = w.shape
    w = f64(np.asarray(w, np.float32).astype(ml_dtypes.bfloat16)).reshape(k // 32, 32, n)
    amax = np.abs(w).max(1)
    if fmt in ("e4m3", "e5m2"):
        byte = np.frexp(amax)[1] - 1 + 127 - (7 if fmt == "e4m3" else 14)
    else:
        mant, ex = np.frexp(amax / 6.0)
        byte = np.where(mant > 0.5, ex, ex - 1) + 127
    byte = np.clip(np.where(amax > 0, byte, 1), 1, 254)
    scaled = (w * np.exp2(127.0 - byte)[:, None, :]).reshape(k, n).astype(np.float32)
    by_word = np.ascontiguousarray(scaled.reshape(k // 512, 128, 4, n).transpose(0, 1, 3, 2))
    if fmt in ("e4m3", "e5m2"):
        words = by_word.astype(ml_dtypes.float8_e4m3fn if fmt == "e4m3" else ml_dtypes.float8_e5m2).view(np.uint8)
    else:
        c = by_word.astype(ml_dtypes.float4_e2m1fn).view(np.uint8) & 0xF
        words = (c[..., 0::2] | (c[..., 1::2] << 4)).reshape(k // 512, 128, 2 * n)
    return np.ascontiguousarray(words), np.ascontiguousarray(byte.astype(np.uint8).reshape(k // 512, 16, n))


def unpack_weight(words, scales, fmt):
    g, _, n = scales.shape
    words = np.ascontiguousarray(words).reshape(g, 128, n, -1)
    if fmt in ("e4m3", "e5m2"):
        vals = words.view(ml_dtypes.float8_e4m3fn if fmt == "e4m3" else ml_dtypes.float8_e5m2).astype(np.float64)
    else:
        nib = np.empty((g, 128, n, 4), np.uint8)
        nib[..., 0::2] = words & 0xF
        nib[..., 1::2] = words >> 4
        vals = E2M1[nib]
    vals = vals * np.repeat(np.exp2(scales.astype(np.float64) - 127.0), 8, axis=1)[..., None]
    return vals.transpose(0, 1, 3, 2).reshape(g * 512, n)


K, T, Z, J, R, N, L, E = 512, 1024, 1024, 256, 512, 256, 512, 128


def setup_inputs():
    n = np.random.standard_normal
    idx = np.random.permutation(T)[:J]
    idx2 = np.random.permutation(Z)[:J]
    idx3 = np.random.permutation(J)[:E]
    idx4 = np.random.permutation(J)[:E]
    fk = mx_kscale(K)
    fr = mx_kscale(R)
    fl = mx_kscale(L)
    xtp = pack_weight(n((K, T)) / fk[:, None], "e2m1")
    xop = pack_weight(n((K, Z)) / fk[:, None], "e5m2")
    wp = pack_weight(n((K, R)) * 1 / np.sqrt(K) * fk[:, None] * fr, "e5m2")
    wbp = pack_weight(n((R, N)) * 1 / np.sqrt(R) / fr[:, None], "e4m3")
    sxp = pack_weight(n((L, J)) / fl[:, None], "e5m2")
    wsp = pack_weight(n((L, N)) * 1 / np.sqrt(L) * fl[:, None], "e4m3")
    return {
        "xt_words": xtp[0],
        "xt_scales": xtp[1],
        "xo_words": xop[0],
        "xo_scales": xop[1],
        "w_words": wp[0],
        "w_scales": wp[1],
        "wb_words": wbp[0],
        "wb_scales": wbp[1],
        "sx_words": sxp[0],
        "sx_scales": sxp[1],
        "ws_words": wsp[0],
        "ws_scales": wsp[1],
        "offs": striped(idx),
        "offs2": striped(idx2),
        "offs3": striped(idx3),
        "offs4": striped(idx4),
    }


def reference(xt_words, xt_scales, xo_words, xo_scales, w_words, w_scales, wb_words, wb_scales, sx_words, sx_scales, ws_words, ws_scales, offs, offs2, offs3, offs4):
    idx = unstriped(offs)
    idx2 = unstriped(offs2)
    idx3 = unstriped(offs3)
    idx4 = unstriped(offs4)
    xtu = unpack_weight(xt_words, xt_scales, "e2m1")
    xou = unpack_weight(xo_words, xo_scales, "e5m2")
    wu = unpack_weight(w_words, w_scales, "e5m2")
    wbu = unpack_weight(wb_words, wb_scales, "e4m3")
    sxu = unpack_weight(sx_words, sx_scales, "e5m2")
    wsu = unpack_weight(ws_words, ws_scales, "e4m3")
    xtidxg = xtu[:, idx]
    a = wu.T @ xtidxg
    xoidx2g = xou[:, idx2]
    b = wu.T @ xoidx2g
    hid = np.maximum(a, b)
    hidq = mxq(hid, 0, "e5m2")
    p = wbu.T @ hidq + wsu.T @ sxu
    y = np.maximum(p[:, idx3], p[:, idx4])
    return y

@@ -1,0 +1,185 @@
+from contextlib import ExitStack
+
+import concourse.mybir as mybir
+
+K, T, Z, J, R, N, L, E = 512, 1024, 1024, 256, 512, 256, 512, 128
+FLOPS = 2 * (2 * K * R * J + R * N * J + L * N * J)
+
+F32 = mybir.dt.float32
+BF16 = mybir.dt.bfloat16
+I32 = mybir.dt.int32
+U32 = mybir.dt.uint32
+U16 = mybir.dt.uint16
+U8 = mybir.dt.uint8
+E2M1 = mybir.dt.float4_e2m1fn_x4
+E5M2 = mybir.dt.float8_e5m2_x4
+E4M3 = mybir.dt.float8_e4m3fn_x4
+COPY = mybir.ActivationFunctionType.Copy
+MAX = mybir.AluOpType.max
+
+P = 128
+PACK = 4
+HALF = 128
+QUAD = 32
+
+
+def load_scale_rows(queue, raw, scales, quadrant, col0, width):
+    dst = raw[QUAD * quadrant : QUAD * quadrant + 4, :].bitcast(I32).rearrange("r (b c) -> r b c", b=2)
+    src = scales[0].bitcast(I32).rearrange("(b q r) c -> q r b c", b=2, q=2)
+    queue.dma_start(out=dst[:, :, col0 // 4 : (col0 + width) // 4], in_=src[quadrant])
+
+
+def lift_scale_rows(nc, raw, total):
+    words = raw[:].bitcast(I32)
+    nc.vector.tensor_copy(out=words[64:128, 0 : total // 4], in_=words[0:64, total // 4 : total // 2])
+
+
+def tile_list_oneforboth_direct_skip_bestoftwo_kernel(
+    tc, xt_words, xt_scales, xo_words, xo_scales, w_words, w_scales, wb_words, wb_scales,
+    sx_words, sx_scales, ws_words, ws_scales, offs, offs2, offs3, offs4, out,
+):
+    nc = tc.nc
+    with ExitStack() as ctx:
+        sb = ctx.enter_context(tc.tile_pool(name="sb", bufs=1))
+        ps = ctx.enter_context(tc.psum_pool(name="ps", bufs=1))
+
+        def tile(name, shape, dtype):
+            return sb.tile(shape, dtype, name=name, align_bytes=64)
+
+        idx = tile("idx", [P, J // 16], U16)
+        idx2 = tile("idx2", [P, J // 16], U16)
+        idx3 = tile("idx3", [P, E // 16], U16)
+        idx4 = tile("idx4", [P, E // 16], U16)
+        xt_w = tile("xt_w", [P, T], U16)
+        xo_w = tile("xo_w", [P, Z], U32)
+        w_w = tile("w_w", [P, R], U32)
+        wb_w = tile("wb_w", [P, N], U32)
+        sx_w = tile("sx_w", [P, J], U32)
+        ws_w = tile("ws_w", [P, N], U32)
+        xt_s = tile("xt_s", [P, 2 * T], U8)
+        xt_sw = tile("xt_sw", [P, T], U8)
+        xo_s = tile("xo_s", [P, Z], U8)
+        w_s = tile("w_s", [P, 2 * R], U8)
+        late = N + J + N
+        late_s = tile("late_s", [P, 2 * late], U8)
+
+        nc.vector.memset(xt_s[0:64, :].bitcast(I32), 0)
+        nc.vector.memset(w_s[0:64, :].bitcast(I32), 0)
+        nc.vector.memset(xo_s[:].bitcast(I32), 0)
+        nc.gpsimd.memset(late_s[0:64, :].bitcast(I32), 0)
+
+        def words(ap):
+            return ap[0].rearrange("p c t -> p (c t)").bitcast(I32)
+
+        nc.sync.dma_start(idx[:], offs)
+        nc.scalar.dma_start(out=xt_w[:].bitcast(I32), in_=xt_words[0].bitcast(I32))
+        nc.scalar.dma_start(out=w_w[:].bitcast(I32), in_=words(w_words))
+        nc.scalar.dma_start(out=xo_w[:].bitcast(I32), in_=words(xo_words))
+        for q in range(2):
+            load_scale_rows(nc.sync, xt_s, xt_scales, q, 0, T)
+        for q in range(2):
+            load_scale_rows(nc.sync, w_s, w_scales, q, 0, R)
+        nc.sync.dma_start(idx2[:], offs2)
+        for q in range(4):
+            nc.sync.dma_start(
+                out=xo_s[QUAD * q : QUAD * q + 4, :].bitcast(I32), in_=xo_scales[0].bitcast(I32)[4 * q : 4 * q + 4, :]
+            )
+        late_inputs = ((ws_scales, 0), (sx_scales, N), (wb_scales, N + J))
+        for scales, col0 in late_inputs:
+            load_scale_rows(nc.gpsimd, late_s, scales, 0, col0, N)
+        for scales, col0 in late_inputs:
+            load_scale_rows(nc.sync, late_s, scales, 1, col0, N)
+        nc.sync.dma_start(out=sx_w[:].bitcast(I32), in_=words(sx_words))
+        nc.sync.dma_start(out=ws_w[:].bitcast(I32), in_=words(ws_words))
+        nc.sync.dma_start(out=wb_w[:].bitcast(I32), in_=words(wb_words))
+        nc.sync.dma_start(idx3[:], offs3)
+        nc.sync.dma_start(idx4[:], offs4)
+
+        wp_w = tile("wp_w", [P, R], U32)
+        wp_s = tile("wp_s", [P, R], U8)
+        nc.scalar.copy(
+            out=wp_w[:].rearrange("p (t c i) -> p c t i", t=PACK, i=4),
+            in_=w_w[:].rearrange("p (c i t) -> p c t i", t=PACK, i=4),
+        )
+        xtg_w = tile("xtg_w", [P, J], U16)
+        xtg_s = tile("xtg_s", [P, J], U8)
+        for b in range(2):
+            nc.vector.tensor_copy(
+                out=xt_sw[64 * b : 64 * (b + 1), :].bitcast(I32), in_=xt_s[0:64, b * T : (b + 1) * T].bitcast(I32)
+            )
+        lift_scale_rows(nc, w_s, R)
+        nc.vector.tensor_copy(out=xtg_w[:], in_=xt_w[:].indirect(idx[:]))
+        nc.vector.tensor_copy(out=xtg_s[:], in_=xt_sw[:].indirect(idx[:]))
+        nc.vector.tensor_copy(
+            out=wp_s[:].rearrange("p (t c i) -> p c t i", t=PACK, i=16),
+            in_=w_s[:, 0:R].rearrange("p (c i t) -> p c t i", t=PACK, i=16),
+        )
+
+        def first_stage(acc, moving, moving_scale):
+            for t in range(PACK):
+                cols = slice(t * P, (t + 1) * P)
+                nc.tensor.matmul_mx(
+                    out=acc[:, t, :], lhsT=wp_w[:, cols].bitcast(E5M2), lhsT_scale=wp_s[:, cols],
+                    rhs=moving, rhs_scale=moving_scale, start=True, stop=True,
+                )
+
+        halves = J // HALF
+        a_sb = []
+        for h in range(halves):
+            cols = slice(h * HALF, (h + 1) * HALF)
+            acc = ps.tile([P, PACK, HALF], F32, name=f"a_ps{h}")
+            first_stage(acc, xtg_w[:, cols].bitcast(E2M1), xtg_s[:, cols])
+            a = tile(f"a_sb{h}", [P, HALF, PACK], F32)
+            nc.scalar.activation(out=a[:], in_=acc[:].rearrange("p t j -> p j t"), func=COPY)
+            a_sb.append(a)
+
+        b_ps = []
+        for h in range(halves):
+            lst = idx2[:, h * HALF // 16 : (h + 1) * HALF // 16]
+            g_s = tile(f"xog_s{h}", [P, HALF], U8)
+            g_w = tile(f"xog_w{h}", [P, HALF], U32)
+            nc.vector.tensor_copy(out=g_s[:], in_=xo_s[:].indirect(lst))
+            nc.vector.tensor_copy(out=g_w[:], in_=xo_w[:].indirect(lst))
+            acc = ps.tile([P, PACK, HALF], F32, name=f"b_ps{h}")
+            first_stage(acc, g_w[:].bitcast(E5M2), g_s[:])
+            b_ps.append(acc)
+
+        hid = []
+        for h in range(halves):
+            hb = tile(f"hid{h}", [P, HALF, PACK], BF16)
+            nc.vector.tensor_tensor(out=hb[:], in0=b_ps[h][:].rearrange("p t j -> p j t"), in1=a_sb[h][:], op=MAX)
+            hid.append(hb)
+            if h == 0:
+                lift_scale_rows(nc, late_s, late)
+
+        p_sb = [tile(f"p_sb{n}", [P, J], F32) for n in range(N // P)]
+        for h in range(halves):
+            cols = slice(h * HALF, (h + 1) * HALF)
+            hq_w = tile(f"hq_w{h}", [P, HALF], U32)
+            hq_s = tile(f"hq_s{h}", [P, HALF], U8)
+            nc.vector.quantize_mx(out=hq_w[:].bitcast(E5M2), scales=hq_s[:], in_=hid[h][:].rearrange("p j t -> p (j t)"))
+            for n in range(N // P):
+                acc = ps.tile([P, HALF], F32, name=f"p_ps{h}{n}")
+                nc.tensor.matmul_mx(
+                    out=acc[:], lhsT=ws_w[:, n * P : (n + 1) * P].bitcast(E4M3), lhsT_scale=late_s[:, n * P : (n + 1) * P],
+                    rhs=sx_w[:, cols].bitcast(E5M2), rhs_scale=late_s[:, N + h * HALF : N + (h + 1) * HALF],
+                    start=True, stop=False,
+                )
+                nc.tensor.matmul_mx(
+                    out=acc[:], lhsT=wb_w[:, n * P : (n + 1) * P].bitcast(E4M3),
+                    lhsT_scale=late_s[:, N + J + n * P : N + J + (n + 1) * P],
+                    rhs=hq_w[:].bitcast(E5M2), rhs_scale=hq_s[:], start=False, stop=True,
+                )
+                if h == halves - 1 and n == 1:
+                    nc.vector.tensor_copy(out=p_sb[n][:, cols], in_=acc[:])
+                else:
+                    nc.scalar.copy(out=p_sb[n][:, cols], in_=acc[:])
+
+        picked = [[tile(f"picked{n}{i}", [P, E], F32) for i in range(2)] for n in range(N // P)]
+        for i, lst in enumerate((idx3, idx4)):
+            nc.scalar.activation(out=picked[0][i][:], in_=p_sb[0][:].indirect(lst[:]), func=COPY)
+            nc.vector.tensor_copy(out=picked[1][i][:], in_=p_sb[1][:].indirect(lst[:]))
+        for n, queue in ((1, nc.sync), (0, nc.scalar)):
+            best = tile(f"best{n}", [P, E], F32)
+            nc.vector.tensor_tensor(out=best[:], in0=picked[n][0][:], in1=picked[n][1][:], op=MAX)
+            queue.dma_start(out=out[n * P : (n + 1) * P, :], in_=best[:])

@@ -43,8 +43,8 @@ def tile_list_oneforboth_direct_skip_bestoftwo_kernel(
         sb = ctx.enter_context(tc.tile_pool(name="sb", bufs=1))
         ps = ctx.enter_context(tc.psum_pool(name="ps", bufs=1))
 
-        def tile(name, shape, dtype):
-            return sb.tile(shape, dtype, name=name, align_bytes=64)
+        def tile(name, shape, dtype, tag=""):
+            return sb.tile(shape, dtype, name=name, tag=tag, align_bytes=64)
 
         idx = tile("idx", [P, J // 16], U16)
         idx2 = tile("idx2", [P, J // 16], U16)
@@ -59,36 +59,39 @@ def tile_list_oneforboth_direct_skip_bestoftwo_kernel(
         xt_s = tile("xt_s", [P, 2 * T], U8)
         xt_sw = tile("xt_sw", [P, T], U8)
         xo_s = tile("xo_s", [P, Z], U8)
-        w_s = tile("w_s", [P, 2 * R], U8)
+        w_s = tile("w_s", [P, 2 * R], U8, tag="w_s")
         late = N + J + N
-        late_s = tile("late_s", [P, 2 * late], U8)
+        late_raw = tile("late_raw", [P, 4 * late], U8, tag="late_raw")
+        late_s = tile("late_s", [P, late], U8)
 
-        nc.vector.memset(xt_s[0:64, :].bitcast(I32), 0)
         nc.vector.memset(w_s[0:64, :].bitcast(I32), 0)
+        nc.gpsimd.memset(xt_s[0:64, T : 2 * T].bitcast(I32), 0)
+        nc.vector.memset(xt_s[0:64, 0:T].bitcast(I32), 0)
         nc.vector.memset(xo_s[:].bitcast(I32), 0)
-        nc.gpsimd.memset(late_s[0:64, :].bitcast(I32), 0)
+        nc.vector.memset(late_s[:].bitcast(I32), 0)
 
         def words(ap):
             return ap[0].rearrange("p c t -> p (c t)").bitcast(I32)
 
         nc.sync.dma_start(idx[:], offs)
-        nc.scalar.dma_start(out=xt_w[:].bitcast(I32), in_=xt_words[0].bitcast(I32))
-        nc.scalar.dma_start(out=w_w[:].bitcast(I32), in_=words(w_words))
-        nc.scalar.dma_start(out=xo_w[:].bitcast(I32), in_=words(xo_words))
-        for q in range(2):
-            load_scale_rows(nc.sync, xt_s, xt_scales, q, 0, T)
+        nc.sync.dma_start(out=xt_w[:].bitcast(I32), in_=xt_words[0].bitcast(I32))
+        nc.sync.dma_start(idx2[:], offs2)
         for q in range(2):
             load_scale_rows(nc.sync, w_s, w_scales, q, 0, R)
-        nc.sync.dma_start(idx2[:], offs2)
+        load_scale_rows(nc.sync, xt_s, xt_scales, 0, 0, T)
+        load_scale_rows(nc.scalar, xt_s, xt_scales, 1, 0, T)
+        nc.sync.dma_start(out=w_w[:].bitcast(I32), in_=words(w_words))
+        nc.sync.dma_start(out=xo_w[:].bitcast(I32), in_=words(xo_words))
         for q in range(4):
             nc.sync.dma_start(
                 out=xo_s[QUAD * q : QUAD * q + 4, :].bitcast(I32), in_=xo_scales[0].bitcast(I32)[4 * q : 4 * q + 4, :]
             )
         late_inputs = ((ws_scales, 0), (sx_scales, N), (wb_scales, N + J))
         for scales, col0 in late_inputs:
-            load_scale_rows(nc.gpsimd, late_s, scales, 0, col0, N)
-        for scales, col0 in late_inputs:
-            load_scale_rows(nc.sync, late_s, scales, 1, col0, N)
+            nc.sync.dma_start(
+                out=late_raw[0:4, :].bitcast(I32).rearrange("r (q c) -> r q c", q=4)[:, :, col0 // 4 : (col0 + N) // 4],
+                in_=scales[0].bitcast(I32).rearrange("(q r) c -> r q c", q=4),
+            )
         nc.sync.dma_start(out=sx_w[:].bitcast(I32), in_=words(sx_words))
         nc.sync.dma_start(out=ws_w[:].bitcast(I32), in_=words(ws_words))
         nc.sync.dma_start(out=wb_w[:].bitcast(I32), in_=words(wb_words))
@@ -102,14 +105,13 @@ def tile_list_oneforboth_direct_skip_bestoftwo_kernel(
             in_=w_w[:].rearrange("p (c i t) -> p c t i", t=PACK, i=4),
         )
         xtg_w = tile("xtg_w", [P, J], U16)
-        xtg_s = tile("xtg_s", [P, J], U8)
+        xtg_s = tile("xtg_s", [P, J], U8, tag="w_s")
+        lift_scale_rows(nc, w_s, R)
         for b in range(2):
             nc.vector.tensor_copy(
                 out=xt_sw[64 * b : 64 * (b + 1), :].bitcast(I32), in_=xt_s[0:64, b * T : (b + 1) * T].bitcast(I32)
             )
-        lift_scale_rows(nc, w_s, R)
         nc.vector.tensor_copy(out=xtg_w[:], in_=xt_w[:].indirect(idx[:]))
-        nc.vector.tensor_copy(out=xtg_s[:], in_=xt_sw[:].indirect(idx[:]))
         nc.vector.tensor_copy(
             out=wp_s[:].rearrange("p (t c i) -> p c t i", t=PACK, i=16),
             in_=w_s[:, 0:R].rearrange("p (c i t) -> p c t i", t=PACK, i=16),
@@ -127,6 +129,9 @@ def tile_list_oneforboth_direct_skip_bestoftwo_kernel(
         a_sb = []
         for h in range(halves):
             cols = slice(h * HALF, (h + 1) * HALF)
+            nc.vector.tensor_copy(
+                out=xtg_s[:, cols], in_=xt_sw[:].indirect(idx[:, h * HALF // 16 : (h + 1) * HALF // 16])
+            )
             acc = ps.tile([P, PACK, HALF], F32, name=f"a_ps{h}")
             first_stage(acc, xtg_w[:, cols].bitcast(E2M1), xtg_s[:, cols])
             a = tile(f"a_sb{h}", [P, HALF, PACK], F32)
@@ -144,42 +149,50 @@ def tile_list_oneforboth_direct_skip_bestoftwo_kernel(
             first_stage(acc, g_w[:].bitcast(E5M2), g_s[:])
             b_ps.append(acc)
 
-        hid = []
+        for q in range(4):
+            nc.vector.tensor_copy(
+                out=late_s[QUAD * q : QUAD * q + 4, :].bitcast(I32),
+                in_=late_raw[0:4, q * late : (q + 1) * late].bitcast(I32),
+            )
+        hid = tile("hid", [P, J * PACK], BF16, tag="late_raw")
         for h in range(halves):
-            hb = tile(f"hid{h}", [P, HALF, PACK], BF16)
-            nc.vector.tensor_tensor(out=hb[:], in0=b_ps[h][:].rearrange("p t j -> p j t"), in1=a_sb[h][:], op=MAX)
-            hid.append(hb)
-            if h == 0:
-                lift_scale_rows(nc, late_s, late)
+            hb = hid[:, h * HALF * PACK : (h + 1) * HALF * PACK]
+            nc.vector.tensor_tensor(out=hb.rearrange("p (j t) -> p j t", t=PACK), in0=b_ps[h][:].rearrange("p t j -> p j t"), in1=a_sb[h][:], op=MAX)
 
         p_sb = [tile(f"p_sb{n}", [P, J], F32) for n in range(N // P)]
+        p_ps = {}
         for h in range(halves):
-            cols = slice(h * HALF, (h + 1) * HALF)
-            hq_w = tile(f"hq_w{h}", [P, HALF], U32)
-            hq_s = tile(f"hq_s{h}", [P, HALF], U8)
-            nc.vector.quantize_mx(out=hq_w[:].bitcast(E5M2), scales=hq_s[:], in_=hid[h][:].rearrange("p j t -> p (j t)"))
             for n in range(N // P):
                 acc = ps.tile([P, HALF], F32, name=f"p_ps{h}{n}")
                 nc.tensor.matmul_mx(
                     out=acc[:], lhsT=ws_w[:, n * P : (n + 1) * P].bitcast(E4M3), lhsT_scale=late_s[:, n * P : (n + 1) * P],
-                    rhs=sx_w[:, cols].bitcast(E5M2), rhs_scale=late_s[:, N + h * HALF : N + (h + 1) * HALF],
+                    rhs=sx_w[:, h * HALF : (h + 1) * HALF].bitcast(E5M2),
+                    rhs_scale=late_s[:, N + h * HALF : N + (h + 1) * HALF],
                     start=True, stop=False,
                 )
+                p_ps[h, n] = acc
+        for h in range(halves):
+            cols = slice(h * HALF, (h + 1) * HALF)
+            hq_w = tile(f"hq_w{h}", [P, HALF], U32)
+            hq_s = tile(f"hq_s{h}", [P, HALF], U8)
+            nc.vector.quantize_mx(out=hq_w[:].bitcast(E5M2), scales=hq_s[:], in_=hid[:, h * HALF * PACK : (h + 1) * HALF * PACK])
+            for n in range(N // P):
+                acc = p_ps[h, n]
                 nc.tensor.matmul_mx(
                     out=acc[:], lhsT=wb_w[:, n * P : (n + 1) * P].bitcast(E4M3),
                     lhsT_scale=late_s[:, N + J + n * P : N + J + (n + 1) * P],
                     rhs=hq_w[:].bitcast(E5M2), rhs_scale=hq_s[:], start=False, stop=True,
                 )
-                if h == halves - 1 and n == 1:
+                if h == halves - 1 and n == 0:
                     nc.vector.tensor_copy(out=p_sb[n][:, cols], in_=acc[:])
                 else:
                     nc.scalar.copy(out=p_sb[n][:, cols], in_=acc[:])
 
         picked = [[tile(f"picked{n}{i}", [P, E], F32) for i in range(2)] for n in range(N // P)]
         for i, lst in enumerate((idx3, idx4)):
-            nc.scalar.activation(out=picked[0][i][:], in_=p_sb[0][:].indirect(lst[:]), func=COPY)
-            nc.vector.tensor_copy(out=picked[1][i][:], in_=p_sb[1][:].indirect(lst[:]))
-        for n, queue in ((1, nc.sync), (0, nc.scalar)):
+            nc.vector.tensor_copy(out=picked[0][i][:], in_=p_sb[0][:].indirect(lst[:]))
+            nc.scalar.activation(out=picked[1][i][:], in_=p_sb[1][:].indirect(lst[:]), func=COPY)
+        for n, queue in ((0, nc.sync), (1, nc.scalar)):
             best = tile(f"best{n}", [P, E], F32)
             nc.vector.tensor_tensor(out=best[:], in0=picked[n][0][:], in1=picked[n][1][:], op=MAX)
             queue.dma_start(out=out[n * P : (n + 1) * P, :], in_=best[:])

@@ -23,10 +23,10 @@ HALF = 128
 QUAD = 32
 
 
-def load_scale_rows(queue, raw, scales, quadrant, col0, width):
-    dst = raw[QUAD * quadrant : QUAD * quadrant + 4, :].bitcast(I32).rearrange("r (b c) -> r b c", b=2)
+def load_scale_rows(queue, raw, scales, quadrant, base):
+    dst = raw[base + QUAD * quadrant : base + QUAD * quadrant + 4, :].bitcast(I32).rearrange("r (b c) -> r b c", b=2)
     src = scales[0].bitcast(I32).rearrange("(b q r) c -> q r b c", b=2, q=2)
-    queue.dma_start(out=dst[:, :, col0 // 4 : (col0 + width) // 4], in_=src[quadrant])
+    queue.dma_start(out=dst, in_=src[quadrant])
 
 
 def lift_scale_rows(nc, raw, total):
@@ -59,14 +59,14 @@ def tile_list_oneforboth_direct_skip_bestoftwo_kernel(
         xt_s = tile("xt_s", [P, 2 * T], U8)
         xt_sw = tile("xt_sw", [P, T], U8)
         xo_s = tile("xo_s", [P, Z], U8)
-        w_s = tile("w_s", [P, 2 * R], U8, tag="w_s")
+        w_s = tile("w_s", [P, 2 * R], U8)
         late = N + J + N
         late_raw = tile("late_raw", [P, 4 * late], U8, tag="late_raw")
         late_s = tile("late_s", [P, late], U8)
 
         nc.vector.memset(w_s[0:64, :].bitcast(I32), 0)
-        nc.gpsimd.memset(xt_s[0:64, T : 2 * T].bitcast(I32), 0)
-        nc.vector.memset(xt_s[0:64, 0:T].bitcast(I32), 0)
+        nc.gpsimd.memset(xt_s[64:128, T : 2 * T].bitcast(I32), 0)
+        nc.vector.memset(xt_s[64:128, 0:T].bitcast(I32), 0)
         nc.vector.memset(xo_s[:].bitcast(I32), 0)
         nc.vector.memset(late_s[:].bitcast(I32), 0)
 
@@ -77,15 +77,13 @@ def tile_list_oneforboth_direct_skip_bestoftwo_kernel(
         nc.sync.dma_start(out=xt_w[:].bitcast(I32), in_=xt_words[0].bitcast(I32))
         nc.sync.dma_start(idx2[:], offs2)
         for q in range(2):
-            load_scale_rows(nc.sync, w_s, w_scales, q, 0, R)
-        load_scale_rows(nc.sync, xt_s, xt_scales, 0, 0, T)
-        load_scale_rows(nc.scalar, xt_s, xt_scales, 1, 0, T)
+            load_scale_rows(nc.sync, w_s, w_scales, q, 0)
+        load_scale_rows(nc.sync, xt_s, xt_scales, 0, 64)
+        load_scale_rows(nc.scalar, xt_s, xt_scales, 1, 64)
         nc.sync.dma_start(out=w_w[:].bitcast(I32), in_=words(w_words))
         nc.sync.dma_start(out=xo_w[:].bitcast(I32), in_=words(xo_words))
-        for q in range(4):
-            nc.sync.dma_start(
-                out=xo_s[QUAD * q : QUAD * q + 4, :].bitcast(I32), in_=xo_scales[0].bitcast(I32)[4 * q : 4 * q + 4, :]
-            )
+        for r in range(4):
+            nc.sync.dma_start(out=xo_s[r:P:QUAD, :].bitcast(I32), in_=xo_scales[0].bitcast(I32)[r:16:4, :])
         late_inputs = ((ws_scales, 0), (sx_scales, N), (wb_scales, N + J))
         for scales, col0 in late_inputs:
             nc.sync.dma_start(
@@ -105,11 +103,11 @@ def tile_list_oneforboth_direct_skip_bestoftwo_kernel(
             in_=w_w[:].rearrange("p (c i t) -> p c t i", t=PACK, i=4),
         )
         xtg_w = tile("xtg_w", [P, J], U16)
-        xtg_s = tile("xtg_s", [P, J], U8, tag="w_s")
+        xtg_s = tile("xtg_s", [P, J], U8)
         lift_scale_rows(nc, w_s, R)
         for b in range(2):
             nc.vector.tensor_copy(
-                out=xt_sw[64 * b : 64 * (b + 1), :].bitcast(I32), in_=xt_s[0:64, b * T : (b + 1) * T].bitcast(I32)
+                out=xt_sw[64 * b : 64 * (b + 1), :].bitcast(I32), in_=xt_s[64:128, b * T : (b + 1) * T].bitcast(I32)
             )
         nc.vector.tensor_copy(out=xtg_w[:], in_=xt_w[:].indirect(idx[:]))
         nc.vector.tensor_copy(
@@ -189,9 +187,9 @@ def tile_list_oneforboth_direct_skip_bestoftwo_kernel(
                     nc.scalar.copy(out=p_sb[n][:, cols], in_=acc[:])
 
         picked = [[tile(f"picked{n}{i}", [P, E], F32) for i in range(2)] for n in range(N // P)]
-        for i, lst in enumerate((idx3, idx4)):
-            nc.vector.tensor_copy(out=picked[0][i][:], in_=p_sb[0][:].indirect(lst[:]))
-            nc.scalar.activation(out=picked[1][i][:], in_=p_sb[1][:].indirect(lst[:]), func=COPY)
+        for n in range(N // P):
+            nc.vector.tensor_copy(out=picked[n][0][:], in_=p_sb[n][:].indirect(idx3[:]))
+            nc.scalar.activation(out=picked[n][1][:], in_=p_sb[n][:].indirect(idx4[:]), func=COPY)
         for n, queue in ((0, nc.sync), (1, nc.scalar)):
             best = tile(f"best{n}", [P, E], F32)
             nc.vector.tensor_tensor(out=best[:], in0=picked[n][0][:], in1=picked[n][1][:], op=MAX)

@@ -65,8 +65,8 @@ def tile_list_oneforboth_direct_skip_bestoftwo_kernel(
         late_s = tile("late_s", [P, late], U8)
 
         nc.vector.memset(w_s[0:64, :].bitcast(I32), 0)
-        nc.gpsimd.memset(xt_s[64:128, T : 2 * T].bitcast(I32), 0)
-        nc.vector.memset(xt_s[64:128, 0:T].bitcast(I32), 0)
+        nc.gpsimd.memset(xt_s[0:64, T : 2 * T].bitcast(I32), 0)
+        nc.vector.memset(xt_s[0:64, 0:T].bitcast(I32), 0)
         nc.vector.memset(xo_s[:].bitcast(I32), 0)
         nc.vector.memset(late_s[:].bitcast(I32), 0)
 
@@ -78,8 +78,8 @@ def tile_list_oneforboth_direct_skip_bestoftwo_kernel(
         nc.sync.dma_start(idx2[:], offs2)
         for q in range(2):
             load_scale_rows(nc.sync, w_s, w_scales, q, 0)
-        load_scale_rows(nc.sync, xt_s, xt_scales, 0, 64)
-        load_scale_rows(nc.scalar, xt_s, xt_scales, 1, 64)
+        load_scale_rows(nc.sync, xt_s, xt_scales, 0, 0)
+        load_scale_rows(nc.scalar, xt_s, xt_scales, 1, 0)
         nc.sync.dma_start(out=w_w[:].bitcast(I32), in_=words(w_words))
         nc.sync.dma_start(out=xo_w[:].bitcast(I32), in_=words(xo_words))
         for r in range(4):
@@ -105,9 +105,9 @@ def tile_list_oneforboth_direct_skip_bestoftwo_kernel(
         xtg_w = tile("xtg_w", [P, J], U16)
         xtg_s = tile("xtg_s", [P, J], U8)
         lift_scale_rows(nc, w_s, R)
-        for b in range(2):
+        for b in (1, 0):
             nc.vector.tensor_copy(
-                out=xt_sw[64 * b : 64 * (b + 1), :].bitcast(I32), in_=xt_s[64:128, b * T : (b + 1) * T].bitcast(I32)
+                out=xt_sw[64 * b : 64 * (b + 1), :].bitcast(I32), in_=xt_s[0:64, b * T : (b + 1) * T].bitcast(I32)
             )
         nc.vector.tensor_copy(out=xtg_w[:], in_=xt_w[:].indirect(idx[:]))
         nc.vector.tensor_copy(

from contextlib import ExitStack

import concourse.mybir as mybir

K, T, Z, J, R, N, L, E = 512, 1024, 1024, 256, 512, 256, 512, 128
FLOPS = 2 * (2 * K * R * J + R * N * J + L * N * J)

F32 = mybir.dt.float32
BF16 = mybir.dt.bfloat16
I32 = mybir.dt.int32
U32 = mybir.dt.uint32
U16 = mybir.dt.uint16
U8 = mybir.dt.uint8
E2M1 = mybir.dt.float4_e2m1fn_x4
E5M2 = mybir.dt.float8_e5m2_x4
E4M3 = mybir.dt.float8_e4m3fn_x4
COPY = mybir.ActivationFunctionType.Copy
MAX = mybir.AluOpType.max

P = 128
PACK = 4
HALF = 128
QUAD = 32


def load_scale_rows(queue, raw, scales, quadrant, base):
    dst = raw[base + QUAD * quadrant : base + QUAD * quadrant + 4, :].bitcast(I32).rearrange("r (b c) -> r b c", b=2)
    src = scales[0].bitcast(I32).rearrange("(b q r) c -> q r b c", b=2, q=2)
    queue.dma_start(out=dst, in_=src[quadrant])


def lift_scale_rows(nc, raw, total):
    words = raw[:].bitcast(I32)
    nc.vector.tensor_copy(out=words[64:128, 0 : total // 4], in_=words[0:64, total // 4 : total // 2])


def tile_list_oneforboth_direct_skip_bestoftwo_kernel(
    tc, xt_words, xt_scales, xo_words, xo_scales, w_words, w_scales, wb_words, wb_scales,
    sx_words, sx_scales, ws_words, ws_scales, offs, offs2, offs3, offs4, out,
):
    nc = tc.nc
    with ExitStack() as ctx:
        sb = ctx.enter_context(tc.tile_pool(name="sb", bufs=1))
        ps = ctx.enter_context(tc.psum_pool(name="ps", bufs=1))

        def tile(name, shape, dtype, tag=""):
            return sb.tile(shape, dtype, name=name, tag=tag, align_bytes=64)

        idx = tile("idx", [P, J // 16], U16)
        idx2 = tile("idx2", [P, J // 16], U16)
        idx3 = tile("idx3", [P, E // 16], U16)
        idx4 = tile("idx4", [P, E // 16], U16)
        xt_w = tile("xt_w", [P, T], U16)
        xo_w = tile("xo_w", [P, Z], U32)
        w_w = tile("w_w", [P, R], U32)
        wb_w = tile("wb_w", [P, N], U32)
        sx_w = tile("sx_w", [P, J], U32)
        ws_w = tile("ws_w", [P, N], U32)
        xt_s = tile("xt_s", [P, 2 * T], U8)
        xt_sw = tile("xt_sw", [P, T], U8)
        xo_s = tile("xo_s", [P, Z], U8)
        w_s = tile("w_s", [P, 2 * R], U8)
        late = N + J + N
        late_raw = tile("late_raw", [P, 4 * late], U8, tag="late_raw")
        late_s = tile("late_s", [P, late], U8)

        nc.vector.memset(w_s[0:64, :].bitcast(I32), 0)
        nc.gpsimd.memset(xt_s[0:64, T : 2 * T].bitcast(I32), 0)
        nc.vector.memset(xt_s[0:64, 0:T].bitcast(I32), 0)
        nc.vector.memset(xo_s[:].bitcast(I32), 0)
        nc.vector.memset(late_s[:].bitcast(I32), 0)

        def words(ap):
            return ap[0].rearrange("p c t -> p (c t)").bitcast(I32)

        nc.sync.dma_start(idx[:], offs)
        nc.sync.dma_start(out=xt_w[:].bitcast(I32), in_=xt_words[0].bitcast(I32))
        nc.sync.dma_start(idx2[:], offs2)
        for q in range(2):
            load_scale_rows(nc.sync, w_s, w_scales, q, 0)
        load_scale_rows(nc.sync, xt_s, xt_scales, 0, 0)
        load_scale_rows(nc.scalar, xt_s, xt_scales, 1, 0)
        nc.sync.dma_start(out=w_w[:].bitcast(I32), in_=words(w_words))
        nc.sync.dma_start(out=xo_w[:].bitcast(I32), in_=words(xo_words))
        for r in range(4):
            nc.sync.dma_start(out=xo_s[r:P:QUAD, :].bitcast(I32), in_=xo_scales[0].bitcast(I32)[r:16:4, :])
        late_inputs = ((ws_scales, 0), (sx_scales, N), (wb_scales, N + J))
        for scales, col0 in late_inputs:
            nc.sync.dma_start(
                out=late_raw[0:4, :].bitcast(I32).rearrange("r (q c) -> r q c", q=4)[:, :, col0 // 4 : (col0 + N) // 4],
                in_=scales[0].bitcast(I32).rearrange("(q r) c -> r q c", q=4),
            )
        nc.sync.dma_start(out=sx_w[:].bitcast(I32), in_=words(sx_words))
        nc.sync.dma_start(out=ws_w[:].bitcast(I32), in_=words(ws_words))
        nc.sync.dma_start(out=wb_w[:].bitcast(I32), in_=words(wb_words))
        nc.sync.dma_start(idx3[:], offs3)
        nc.sync.dma_start(idx4[:], offs4)

        wp_w = tile("wp_w", [P, R], U32)
        wp_s = tile("wp_s", [P, R], U8)
        nc.scalar.copy(
            out=wp_w[:].rearrange("p (t c i) -> p c t i", t=PACK, i=4),
            in_=w_w[:].rearrange("p (c i t) -> p c t i", t=PACK, i=4),
        )
        xtg_w = tile("xtg_w", [P, J], U16)
        xtg_s = tile("xtg_s", [P, J], U8)
        lift_scale_rows(nc, w_s, R)
        for b in (1, 0):
            nc.vector.tensor_copy(
                out=xt_sw[64 * b : 64 * (b + 1), :].bitcast(I32), in_=xt_s[0:64, b * T : (b + 1) * T].bitcast(I32)
            )
        nc.vector.tensor_copy(out=xtg_w[:], in_=xt_w[:].indirect(idx[:]))
        nc.vector.tensor_copy(
            out=wp_s[:].rearrange("p (t c i) -> p c t i", t=PACK, i=16),
            in_=w_s[:, 0:R].rearrange("p (c i t) -> p c t i", t=PACK, i=16),
        )

        def first_stage(acc, moving, moving_scale):
            for t in range(PACK):
                cols = slice(t * P, (t + 1) * P)
                nc.tensor.matmul_mx(
                    out=acc[:, t, :], lhsT=wp_w[:, cols].bitcast(E5M2), lhsT_scale=wp_s[:, cols],
                    rhs=moving, rhs_scale=moving_scale, start=True, stop=True,
                )

        halves = J // HALF
        a_sb = []
        for h in range(halves):
            cols = slice(h * HALF, (h + 1) * HALF)
            nc.vector.tensor_copy(
                out=xtg_s[:, cols], in_=xt_sw[:].indirect(idx[:, h * HALF // 16 : (h + 1) * HALF // 16])
            )
            acc = ps.tile([P, PACK, HALF], F32, name=f"a_ps{h}")
            first_stage(acc, xtg_w[:, cols].bitcast(E2M1), xtg_s[:, cols])
            a = tile(f"a_sb{h}", [P, HALF, PACK], F32)
            nc.scalar.activation(out=a[:], in_=acc[:].rearrange("p t j -> p j t"), func=COPY)
            a_sb.append(a)

        b_ps = []
        for h in range(halves):
            lst = idx2[:, h * HALF // 16 : (h + 1) * HALF // 16]
            g_s = tile(f"xog_s{h}", [P, HALF], U8)
            g_w = tile(f"xog_w{h}", [P, HALF], U32)
            nc.vector.tensor_copy(out=g_s[:], in_=xo_s[:].indirect(lst))
            nc.vector.tensor_copy(out=g_w[:], in_=xo_w[:].indirect(lst))
            acc = ps.tile([P, PACK, HALF], F32, name=f"b_ps{h}")
            first_stage(acc, g_w[:].bitcast(E5M2), g_s[:])
            b_ps.append(acc)

        for q in range(4):
            nc.vector.tensor_copy(
                out=late_s[QUAD * q : QUAD * q + 4, :].bitcast(I32),
                in_=late_raw[0:4, q * late : (q + 1) * late].bitcast(I32),
            )
        hid = tile("hid", [P, J * PACK], BF16, tag="late_raw")
        for h in range(halves):
            hb = hid[:, h * HALF * PACK : (h + 1) * HALF * PACK]
            nc.vector.tensor_tensor(out=hb.rearrange("p (j t) -> p j t", t=PACK), in0=b_ps[h][:].rearrange("p t j -> p j t"), in1=a_sb[h][:], op=MAX)

        p_sb = [tile(f"p_sb{n}", [P, J], F32) for n in range(N // P)]
        p_ps = {}
        for h in range(halves):
            for n in range(N // P):
                acc = ps.tile([P, HALF], F32, name=f"p_ps{h}{n}")
                nc.tensor.matmul_mx(
                    out=acc[:], lhsT=ws_w[:, n * P : (n + 1) * P].bitcast(E4M3), lhsT_scale=late_s[:, n * P : (n + 1) * P],
                    rhs=sx_w[:, h * HALF : (h + 1) * HALF].bitcast(E5M2),
                    rhs_scale=late_s[:, N + h * HALF : N + (h + 1) * HALF],
                    start=True, stop=False,
                )
                p_ps[h, n] = acc
        for h in range(halves):
            cols = slice(h * HALF, (h + 1) * HALF)
            hq_w = tile(f"hq_w{h}", [P, HALF], U32)
            hq_s = tile(f"hq_s{h}", [P, HALF], U8)
            nc.vector.quantize_mx(out=hq_w[:].bitcast(E5M2), scales=hq_s[:], in_=hid[:, h * HALF * PACK : (h + 1) * HALF * PACK])
            for n in range(N // P):
                acc = p_ps[h, n]
                nc.tensor.matmul_mx(
                    out=acc[:], lhsT=wb_w[:, n * P : (n + 1) * P].bitcast(E4M3),
                    lhsT_scale=late_s[:, N + J + n * P : N + J + (n + 1) * P],
                    rhs=hq_w[:].bitcast(E5M2), rhs_scale=hq_s[:], start=False, stop=True,
                )
                if h == halves - 1 and n == 0:
                    nc.vector.tensor_copy(out=p_sb[n][:, cols], in_=acc[:])
                else:
                    nc.scalar.copy(out=p_sb[n][:, cols], in_=acc[:])

        picked = [[tile(f"picked{n}{i}", [P, E], F32) for i in range(2)] for n in range(N // P)]
        for n in range(N // P):
            nc.vector.tensor_copy(out=picked[n][0][:], in_=p_sb[n][:].indirect(idx3[:]))
            nc.scalar.activation(out=picked[n][1][:], in_=p_sb[n][:].indirect(idx4[:]), func=COPY)
        for n, queue in ((0, nc.sync), (1, nc.scalar)):
            best = tile(f"best{n}", [P, E], F32)
            nc.vector.tensor_tensor(out=best[:], in0=picked[n][0][:], in1=picked[n][1][:], op=MAX)
            queue.dma_start(out=out[n * P : (n + 1) * P, :], in_=best[:])
